import numpy as np, ml_dtypes
CORES = [1,2,5,7,57,58,61,63,73,74,77,79]
N = 12
import mx_ref
NC, G = 256, 4
BF = ml_dtypes.bfloat16
def cut(t, i, w=512):
    return t[:, w * i:w * i + w]
def tile(rs):
    return np.stack(rs, axis=2).reshape(128, -1).astype(BF)
def layer(w, X):
    out = []
    for i in range(G):
        for t in range(len(X)):
            p = mx_ref.matmul(mx_ref.quantize(cut(w, len(X) * i + t)), X[t])
            z = p if t == 0 else z + p
        out.append(z)
    return out
def scaled(Z, s):
    return [z * s for z in Z]
def setup_inputs(rng):
    def f(*shape):
        return mx_ref.flush((rng.standard_normal(shape, dtype=np.float32) * np.exp2(rng.integers(-2, 3, shape[:-1] + (1,)))).astype(BF))
    return {"x": f(N, 128, 4 * NC), "w1": f(N, 128, G * 512), "w2": f(N, 128, 2 * 512)}
def setup_inputs_blocks(rng):
    d = setup_inputs(rng)
    for k in ("w2",): d[k] = mx_ref.spread(d[k], rng, 4)
    for k in ("x", "w1"): d[k] = mx_ref.spread(d[k], rng, 2)
    return d
def setup_inputs_wide(rng):
    d = setup_inputs(rng)
    for k in ("x", "w1", "w2"): d[k] = mx_ref.flush((d[k].astype(np.float32) * np.exp2(rng.integers(-3, 4, (N, 1, 1))).astype(np.float32)).astype(BF))
    return d
def reference(x, w1, w2, own=None):
    Z = [layer(w1[r], [mx_ref.quantize(x[r])]) for r in range(N)]
    a = max(float(np.abs(z).max()) for r in range(N) for z in Z[r])
    s = np.float32(1 / a)
    h = np.stack([tile(scaled(Z[r], s)) for r in range(N)])
    use = h if own is None else own["h"]
    H = [mx_ref.quantize(use[j]) for j in range(N)]
    y = np.zeros((N, 128, NC), np.float32)
    for r in range(N):
        y[r] = mx_ref.matmul(mx_ref.quantize(cut(w2[r], 0)), H[r]) + mx_ref.matmul(mx_ref.quantize(cut(w2[r], 1)), H[(r + 1) % N])
    return {"h": h, "y": y}

@@ -1,0 +1,216 @@
+from concourse.bass import DstId, RemoteDMATransfer
+from concourse.mybir import dt, AluOpType, AxisListType, ActivationFunctionType
+
+F8, U8, F32, BF = "float8_e4m3fn_x4", "uint8", "float32", "bfloat16"
+SCRATCH = {
+    "xt": ("sbuf", [128, 1024], BF), "w1t": ("sbuf", [128, 2048], BF), "w2t": ("sbuf", [128, 1024], BF),
+    "xq": ("sbuf", [128, 256], F8), "xs": ("sbuf", [128, 256], U8),
+    "wq": ("sbuf", [128, 512], F8), "ws": ("sbuf", [128, 512], U8),
+    "vq": ("sbuf", [128, 256], F8), "vs": ("sbuf", [128, 256], U8),
+    "ones": ("sbuf", [128, 128], F32), "ident": ("sbuf", [128, 128], F32),
+    "tops": ("sbuf", [128, 16], F32),
+    "cm": ("sbuf", [128, 1], F32),
+    "land": ("sbuf", [128, 4], F32),
+    "rep": ("sbuf", [128, 128], F32), "rep2": ("sbuf", [128, 128], F32),
+    "amax": ("sbuf", [128, 1], F32), "sc": ("sbuf", [128, 1], F32),
+    "ht": ("sbuf", [128, 1024], BF),
+    "hq": ("sbuf", [128, 256], F8), "hs": ("sbuf", [128, 256], U8),
+    "nq": ("sbuf", [128, 256], F8), "ns": ("sbuf", [128, 256], U8),
+    "rq": ("sbuf", [128, 128], F8), "rs": ("sbuf", [128, 128], U8),
+    "yt": ("sbuf", [128, 256], F32),
+    "z": ("psum", [128, 2048], F32), "tp": ("psum", [128, 512], F32), "yp": ("psum", [128, 1024], F32),
+}
+SEMAPHORES = (["ldx", "ldwa", "ldwb", "ldv", "ones", "id", "qx", "cm", "rep", "rep2", "tp", "am", "sc", "qh", "ya", "yb", "ca", "cb",
+               "hout", "yout", "go1", "go2", "a1", "aon", "aoff", "arel", "an", "sent"]
+              + ["qw%d" % i for i in range(4)] + ["z%d" % i for i in range(4)] + ["r%d" % i for i in range(4)]
+              + ["qv%d" % i for i in range(2)] + ["h%d" % i for i in range(4)])
+
+
+def bits(mask):
+    return [1 << i for i in range(mask.bit_length()) if mask >> i & 1]
+
+
+def plan(T, topo):
+    cores = list(T.cores)
+    chips = []
+    for c in cores:
+        if topo.chip(c) not in chips:
+            chips.append(topo.chip(c))
+    on = {k: [c for c in cores if topo.chip(c) == k] for k in chips}
+    ports = {k: [c for c in on[k] if all(topo.may_write(c, d) for d in cores if topo.chip(d) != k)] for k in chips}
+    tells = {c: [] for c in cores}
+    for k in chips:
+        for d in cores:
+            if d in ports[k]:
+                continue
+            best = min(ports[k], key=lambda p: (topo.die(p) != topo.die(d), len(tells[p])))
+            tells[best].append(d)
+    ways = {}
+    for i, c in enumerate(cores):
+        d = cores[i - 1]
+        ways[c] = (d, [] if topo.may_write(c, d) else ports[topo.chip(c)])
+    return cores, chips, on, ports, tells, ways
+
+
+def rank_program(g, core, T, topo):
+    rank = T.rank_of(core)
+    if rank is None:
+        return
+    cores, chips, on, ports, tells, ways = plan(T, topo)
+    S = T.sem
+    home = topo.chip(core)
+    port = core in ports[home]
+    k4 = 4 * on[home].index(core)
+    abroad = [k for k in chips if k != home]
+    far = bits(topo.mask(core, [c for c in cores if topo.chip(c) != home][0]))
+    E = len(far)
+    ALL = sum(far)
+    MAX = AluOpType.max
+    X = AxisListType.X
+    sent = [0]
+
+    def dst(c):
+        rid, pid, _ = topo.addr(c)
+        return DstId(rid=rid, pnc=pid)
+
+    def send(transfers):
+        g.remote_dma_fused([RemoteDMATransfer(dst_ids=[dst(c) for c, _ in outs], dma_engine_mask=sum(eng), remote_sem=sem,
+                                              srcs=[src], dsts=[v for _, v in outs]) for src, outs, eng, sem in transfers], local_sem=S.sent)
+        sent[0] += sum(len(eng) for _, _, eng, _ in transfers)
+
+    def u8(v):
+        return v.bitcast(dt.uint8)
+
+    g.sync.dma_start(T.xt[:], T.x[:]).then_inc(S.ldx, 16)
+    g.scalar.dma_start(T.w1t[:, 0:1024], T.w1[:, 0:1024]).then_inc(S.ldwa, 16)
+    g.sync.dma_start(T.w1t[:, 1024:2048], T.w1[:, 1024:2048]).then_inc(S.ldwb, 16)
+
+    g.vector.memset(T.ones[:], 1.0).then_inc(S.ones, 1)
+    g.wait_ge(S.ones, 1)
+    g.affine_select(T.ident[:], T.ones[:], [[-1, 128]], AluOpType.is_equal, 0.0, 0, 1).then_inc(S.id, 1)
+
+    g.vector.wait_ge(S.ldx, 16)
+    g.vector.quantize_mx(T.xq[:], T.xs[:], T.xt[:]).then_inc(S.qx, 1)
+    g.tensor.wait_ge(S.qx, 1)
+    for half in range(2):
+        g.vector.wait_ge(S.ldwb if half else S.ldwa, 16)
+        for i in (2 * half, 2 * half + 1):
+            a, b = 128 * i, 128 * i + 128
+            g.vector.quantize_mx(T.wq[:, a:b], T.ws[:, a:b], T.w1t[:, 4 * a:4 * b]).then_inc(S["qw%d" % i], 1)
+            g.tensor.wait_ge(S["qw%d" % i], 1)
+            g.tensor.matmul_mx(T.z[:, 512 * i:512 * i + 256], T.wq[:, a:b], T.ws[:, a:b], T.xq[:], T.xs[:], True, True).then_inc(S["z%d" % i], 1)
+        for i in (2 * half, 2 * half + 1):
+            g.vector.wait_ge(S["z%d" % i], 1)
+            g.vector.tensor_reduce(T.tops[:, k4 + i:k4 + i + 1], T.z[:, 512 * i:512 * i + 256], X, MAX,
+                                   apply_absolute_value=True).then_inc(S["r%d" % i], 1)
+
+    for half in range(2):
+        for i in (2 * half, 2 * half + 1):
+            g.wait_ge(S["r%d" % i], 1)
+        v = T.tops[:, k4 + 2 * half:k4 + 2 * half + 2]
+        send([(v, [(p, v) for p in ports[home] if p != core], far, S.a1)])
+    g.sem_inc(S.go1, 1)
+
+    ci = chips.index(home)
+    if port:
+        for i in range(4):
+            g.vector.wait_ge(S["r%d" % i], 1)
+        g.vector.wait_ge(S.a1, 2 * E * (len(on[home]) - 1))
+        g.vector.tensor_reduce(T.cm[:], T.tops[:, 0:4 * len(on[home])], X, MAX).then_inc(S.cm, 1)
+        g.wait_ge(S.cm, 1)
+        send([(T.cm[:], [(d, T.land[:, ci:ci + 1]) for d in sorted(tells[core], key=lambda d: topo.chip(d) == home)
+                         if topo.chip(d) != home], far, S.aoff)])
+        near = [d for d in tells[core] if topo.chip(d) == home]
+        if near:
+            send([(T.cm[:], [(d, T.land[:, ci:ci + 1]) for d in near], far, S.aon)])
+
+    g.sync.wait_ge(S.go1, 1)
+    g.sync.dma_start(T.w2t[:], T.w2[:]).then_inc(S.ldv, 16)
+
+    def quantise_w2():
+        g.vector.wait_ge(S.ldv, 16)
+        for i in range(2):
+            g.vector.quantize_mx(T.vq[:, 128 * i:128 * i + 128], T.vs[:, 128 * i:128 * i + 128],
+                                 T.w2t[:, 512 * i:512 * i + 512]).then_inc(S["qv%d" % i], 1)
+
+    g.vector.wait_ge(S.ones, 1)
+    if port:
+        g.vector.wait_ge(S.cm, 1)
+        g.vector.tensor_scalar(T.rep[:], T.ones[:], T.cm[:], None, AluOpType.mult).then_inc(S.rep, 1)
+        quantise_w2()
+    else:
+        quantise_w2()
+        g.vector.wait_ge(S.aon, E)
+        g.vector.tensor_scalar(T.rep[:], T.ones[:], T.land[:, ci:ci + 1], None, AluOpType.mult).then_inc(S.rep, 1)
+    g.vector.wait_ge(S.rep, 1)
+    g.vector.wait_ge(S.aoff, E * len(abroad))
+    c0, c1 = [chips.index(k) for k in abroad]
+    g.vector.tensor_scalar(T.rep2[:], T.rep[:], T.land[:, c0:c0 + 1], T.land[:, c1:c1 + 1], MAX, MAX).then_inc(S.rep2, 1)
+    g.tensor.wait_ge(S.id, 1)
+    g.tensor.wait_ge(S.rep2, 1)
+    g.tensor.transpose(T.tp[:, 0:128], T.rep2[:], T.ident[:]).then_inc(S.tp, 1)
+    g.vector.wait_ge(S.tp, 1)
+    g.vector.tensor_reduce(T.amax[:], T.tp[:, 0:128], X, MAX).then_inc(S.am, 1)
+    g.vector.wait_ge(S.am, 1)
+    g.vector.reciprocal(T.sc[:], T.amax[:]).then_inc(S.sc, 1)
+
+    g.scalar.wait_ge(S.sc, 1)
+    g.vector.wait_ge(S.sc, 1)
+    for b in range(4):
+        if b < 2:
+            g.vector.tensor_scalar(T.ht[:, b:1024:4], T.z[:, 512 * b:512 * b + 256], T.sc[:], None, AluOpType.mult).then_inc(S["h%d" % b], 1)
+        else:
+            for i in (b,):
+                g.scalar.wait_ge(S["z%d" % i], 1)
+            g.scalar.activation(T.ht[:, b:1024:4], T.z[:, 512 * b:512 * b + 256], ActivationFunctionType.Copy,
+                                scale=T.sc[:]).then_inc(S["h%d" % b], 1)
+    for b in range(4):
+        g.vector.wait_ge(S["h%d" % b], 1)
+    g.vector.quantize_mx(T.hq[:], T.hs[:], T.ht[:]).then_inc(S.qh, 1)
+
+    g.wait_ge(S.qh, 1)
+    to, relays = ways[core]
+    if not relays:
+        send([(u8(T.hq[:]), [(to, u8(T.nq[:]))], far, S.an)])
+        send([(T.hs[:], [(to, T.ns[:])], far, S.an)])
+    else:
+        R = len(relays)
+        w = 256 // R
+        cut = [(j * w, j * w + w, p, far[j::R]) for j, p in enumerate(relays)]
+        send([(u8(T.hq[:, a:b]), [(p, u8(T.rq[:]))], eng, S.arel) for a, b, p, eng in cut])
+        send([(T.hs[:, a:b], [(p, T.rs[:])], eng, S.arel) for a, b, p, eng in cut])
+    for c in on[home]:
+        d, rel = ways[c]
+        if core in rel:
+            j, w = rel.index(core), 256 // len(rel)
+            g.wait_ge(S.arel, 2 * (E // len(rel)))
+            send([(u8(T.rq[:]), [(d, u8(T.nq[:, j * w:j * w + w]))], far, S.an)])
+            send([(T.rs[:], [(d, T.ns[:, j * w:j * w + w])], far, S.an)])
+    g.sem_inc(S.go2, 1)
+    g.wait_ge(S.sent, sent[0])
+
+    g.sync.wait_ge(S.qh, 1)
+    g.sync.wait_ge(S.go2, 1)
+    g.sync.dma_start(T.h[:], T.ht[:]).then_inc(S.hout, 16)
+    g.sync.wait_ge(S.hout, 16)
+
+    g.tensor.wait_ge(S.qh, 1)
+    g.tensor.wait_ge(S.qv0, 1)
+    for j in range(2):
+        a, b = 128 * j, 128 * j + 128
+        g.tensor.matmul_mx(T.yp[:, 512 * j:512 * j + 128], T.vq[:, 0:128], T.vs[:, 0:128], T.hq[:, a:b], T.hs[:, a:b], True, False)
+    g.tensor.wait_ge(S.qv1, 1)
+    prev = cores[(rank + 1) % len(cores)]
+    g.tensor.wait_ge(S.an, 2 * E * max(1, len(ways[prev][1])))
+    for j, name in ((0, "ya"), (1, "yb")):
+        a, b = 128 * j, 128 * j + 128
+        g.tensor.matmul_mx(T.yp[:, 512 * j:512 * j + 128], T.vq[:, 128:256], T.vs[:, 128:256], T.nq[:, a:b], T.ns[:, a:b],
+                           False, True).then_inc(S[name], 1)
+    g.vector.wait_ge(S.ya, 1)
+    g.vector.tensor_copy(T.yt[:, 0:128], T.yp[:, 0:128]).then_inc(S.ca, 1)
+    g.scalar.wait_ge(S.yb, 1)
+    g.scalar.activation(T.yt[:, 128:256], T.yp[:, 512:640], ActivationFunctionType.Copy).then_inc(S.cb, 1)
+    g.scalar.wait_ge(S.ca, 1)
+    g.scalar.wait_ge(S.cb, 1)
+    g.scalar.dma_start(T.y[:], T.yt[:]).then_inc(S.yout, 16)
+    g.scalar.wait_ge(S.yout, 16)

@@ -1,6 +1,9 @@
 from concourse.bass import DstId, RemoteDMATransfer
 from concourse.mybir import dt, AluOpType, AxisListType, ActivationFunctionType
 
+LOADS = [(0, 1), (2, 3)]
+PARTS = [(0, 1), (2, 3)]
+
 F8, U8, F32, BF = "float8_e4m3fn_x4", "uint8", "float32", "bfloat16"
 SCRATCH = {
     "xt": ("sbuf", [128, 1024], BF), "w1t": ("sbuf", [128, 2048], BF), "w2t": ("sbuf", [128, 1024], BF),
@@ -20,10 +23,9 @@ SCRATCH = {
     "yt": ("sbuf", [128, 256], F32),
     "z": ("psum", [128, 2048], F32), "tp": ("psum", [128, 512], F32), "yp": ("psum", [128, 1024], F32),
 }
-SEMAPHORES = (["ldx", "ldwa", "ldwb", "ldv", "ones", "id", "qx", "cm", "rep", "rep2", "tp", "am", "sc", "qh", "ya", "yb", "ca", "cb",
-               "hout", "yout", "go1", "go2", "a1", "aon", "aoff", "arel", "an", "sent"]
-              + ["qw%d" % i for i in range(4)] + ["z%d" % i for i in range(4)] + ["r%d" % i for i in range(4)]
-              + ["qv%d" % i for i in range(2)] + ["h%d" % i for i in range(4)])
+SEMAPHORES = (["ldx", "ldv", "ones", "id", "qx", "cm", "rep", "rep2", "tp", "am", "sc", "qh", "ya", "yb", "ca", "cb",
+               "hout", "yout", "go1", "go2", "a1", "aon", "aoff", "arelq", "arels", "an", "sent"]
+              + [s + "%d" % i for s in ("ldw", "qw", "z", "r", "h", "qv") for i in range(4)])
 
 
 def bits(mask):
@@ -63,9 +65,10 @@ def rank_program(g, core, T, topo):
     k4 = 4 * on[home].index(core)
     abroad = [k for k in chips if k != home]
     far = bits(topo.mask(core, [c for c in cores if topo.chip(c) != home][0]))
-    E = len(far)
-    ALL = sum(far)
-    MAX = AluOpType.max
+    near = bits(topo.mask(core, [c for c in on[home] if c != core][0]))
+    rest = [e for e in near if e not in far]
+    E, NE = len(far), len(near)
+    MAX, MULT = AluOpType.max, AluOpType.mult
     X = AxisListType.X
     sent = [0]
 
@@ -78,12 +81,17 @@ def rank_program(g, core, T, topo):
                                               srcs=[src], dsts=[v for _, v in outs]) for src, outs, eng, sem in transfers], local_sem=S.sent)
         sent[0] += sum(len(eng) for _, _, eng, _ in transfers)
 
+    def way_engines(c):
+        m = bits(topo.mask(c, ways[c][0]))
+        return [e for e in m if e not in far] if c in ports[topo.chip(c)] and len(m) > E else m
+
     def u8(v):
         return v.bitcast(dt.uint8)
 
     g.sync.dma_start(T.xt[:], T.x[:]).then_inc(S.ldx, 16)
-    g.scalar.dma_start(T.w1t[:, 0:1024], T.w1[:, 0:1024]).then_inc(S.ldwa, 16)
-    g.sync.dma_start(T.w1t[:, 1024:2048], T.w1[:, 1024:2048]).then_inc(S.ldwb, 16)
+    for n, grp in enumerate(LOADS):
+        a, b = 512 * grp[0], 512 * grp[-1] + 512
+        (g.sync if n % 2 else g.scalar).dma_start(T.w1t[:, a:b], T.w1[:, a:b]).then_inc(S["ldw%d" % n], 16)
 
     g.vector.memset(T.ones[:], 1.0).then_inc(S.ones, 1)
     g.wait_ge(S.ones, 1)
@@ -92,37 +100,48 @@ def rank_program(g, core, T, topo):
     g.vector.wait_ge(S.ldx, 16)
     g.vector.quantize_mx(T.xq[:], T.xs[:], T.xt[:]).then_inc(S.qx, 1)
     g.tensor.wait_ge(S.qx, 1)
-    for half in range(2):
-        g.vector.wait_ge(S.ldwb if half else S.ldwa, 16)
-        for i in (2 * half, 2 * half + 1):
+
+    def largest(i):
+        g.vector.wait_ge(S["z%d" % i], 1)
+        g.vector.tensor_reduce(T.tops[:, k4 + i:k4 + i + 1], T.z[:, 512 * i:512 * i + 256], X, MAX,
+                               apply_absolute_value=True).then_inc(S["r%d" % i], 1)
+
+    late = []
+    for n, grp in enumerate(LOADS):
+        g.vector.wait_ge(S["ldw%d" % n], 16)
+        for i in grp:
             a, b = 128 * i, 128 * i + 128
             g.vector.quantize_mx(T.wq[:, a:b], T.ws[:, a:b], T.w1t[:, 4 * a:4 * b]).then_inc(S["qw%d" % i], 1)
             g.tensor.wait_ge(S["qw%d" % i], 1)
             g.tensor.matmul_mx(T.z[:, 512 * i:512 * i + 256], T.wq[:, a:b], T.ws[:, a:b], T.xq[:], T.xs[:], True, True).then_inc(S["z%d" % i], 1)
-        for i in (2 * half, 2 * half + 1):
-            g.vector.wait_ge(S["z%d" % i], 1)
-            g.vector.tensor_reduce(T.tops[:, k4 + i:k4 + i + 1], T.z[:, 512 * i:512 * i + 256], X, MAX,
-                                   apply_absolute_value=True).then_inc(S["r%d" % i], 1)
+            late.append(i)
+        while late and (len(grp) > 1 or len(late) > 1):
+            largest(late.pop(0))
+    for i in late:
+        largest(i)
 
-    for half in range(2):
-        for i in (2 * half, 2 * half + 1):
+    for grp in PARTS:
+        for i in grp:
             g.wait_ge(S["r%d" % i], 1)
-        v = T.tops[:, k4 + 2 * half:k4 + 2 * half + 2]
-        send([(v, [(p, v) for p in ports[home] if p != core], far, S.a1)])
-    g.sem_inc(S.go1, 1)
+        v = T.tops[:, k4 + grp[0]:k4 + grp[-1] + 1]
+        send([(v, [(p, v) for p in ports[home] if p != core], near, S.a1)])
 
     ci = chips.index(home)
     if port:
         for i in range(4):
             g.vector.wait_ge(S["r%d" % i], 1)
-        g.vector.wait_ge(S.a1, 2 * E * (len(on[home]) - 1))
+        g.vector.wait_ge(S.a1, len(PARTS) * NE * (len(on[home]) - 1))
         g.vector.tensor_reduce(T.cm[:], T.tops[:, 0:4 * len(on[home])], X, MAX).then_inc(S.cm, 1)
         g.wait_ge(S.cm, 1)
-        send([(T.cm[:], [(d, T.land[:, ci:ci + 1]) for d in sorted(tells[core], key=lambda d: topo.chip(d) == home)
-                         if topo.chip(d) != home], far, S.aoff)])
-        near = [d for d in tells[core] if topo.chip(d) == home]
-        if near:
-            send([(T.cm[:], [(d, T.land[:, ci:ci + 1]) for d in near], far, S.aon)])
+        col = T.land[:, ci:ci + 1]
+        off = [d for d in tells[core] if topo.chip(d) != home]
+        first = [d for d in off if ways[d][1]]
+        here = [(T.cm[:], [(d, col)], rest, S.aon) for d in tells[core] if topo.chip(d) == home]
+        for some in (first, [d for d in off if d not in first]):
+            if some:
+                send([(T.cm[:], [(d, col) for d in some], far, S.aoff)] + here)
+                here = []
+    g.sem_inc(S.go1, 1)
 
     g.sync.wait_ge(S.go1, 1)
     g.sync.dma_start(T.w2t[:], T.w2[:]).then_inc(S.ldv, 16)
@@ -136,12 +155,11 @@ def rank_program(g, core, T, topo):
     g.vector.wait_ge(S.ones, 1)
     if port:
         g.vector.wait_ge(S.cm, 1)
-        g.vector.tensor_scalar(T.rep[:], T.ones[:], T.cm[:], None, AluOpType.mult).then_inc(S.rep, 1)
-        quantise_w2()
+        g.vector.tensor_scalar(T.rep[:], T.ones[:], T.cm[:], None, MULT).then_inc(S.rep, 1)
     else:
         quantise_w2()
-        g.vector.wait_ge(S.aon, E)
-        g.vector.tensor_scalar(T.rep[:], T.ones[:], T.land[:, ci:ci + 1], None, AluOpType.mult).then_inc(S.rep, 1)
+        g.vector.wait_ge(S.aon, len(rest))
+        g.vector.tensor_scalar(T.rep[:], T.ones[:], T.land[:, ci:ci + 1], None, MULT).then_inc(S.rep, 1)
     g.vector.wait_ge(S.rep, 1)
     g.vector.wait_ge(S.aoff, E * len(abroad))
     c0, c1 = [chips.index(k) for k in abroad]
@@ -154,37 +172,40 @@ def rank_program(g, core, T, topo):
     g.vector.wait_ge(S.am, 1)
     g.vector.reciprocal(T.sc[:], T.amax[:]).then_inc(S.sc, 1)
 
+    for b in range(2, 4):
+        g.scalar.wait_ge(S["z%d" % b], 1)
     g.scalar.wait_ge(S.sc, 1)
     g.vector.wait_ge(S.sc, 1)
-    for b in range(4):
-        if b < 2:
-            g.vector.tensor_scalar(T.ht[:, b:1024:4], T.z[:, 512 * b:512 * b + 256], T.sc[:], None, AluOpType.mult).then_inc(S["h%d" % b], 1)
-        else:
-            for i in (b,):
-                g.scalar.wait_ge(S["z%d" % i], 1)
-            g.scalar.activation(T.ht[:, b:1024:4], T.z[:, 512 * b:512 * b + 256], ActivationFunctionType.Copy,
-                                scale=T.sc[:]).then_inc(S["h%d" % b], 1)
+    for b in range(2):
+        g.vector.tensor_scalar(T.ht[:, b:1024:4], T.z[:, 512 * b:512 * b + 256], T.sc[:], None, MULT).then_inc(S["h%d" % b], 1)
+    for b in range(2, 4):
+        g.scalar.activation(T.ht[:, b:1024:4], T.z[:, 512 * b:512 * b + 256], ActivationFunctionType.Copy,
+                            scale=T.sc[:]).then_inc(S["h%d" % b], 1)
     for b in range(4):
         g.vector.wait_ge(S["h%d" % b], 1)
     g.vector.quantize_mx(T.hq[:], T.hs[:], T.ht[:]).then_inc(S.qh, 1)
+    if port:
+        quantise_w2()
 
     g.wait_ge(S.qh, 1)
     to, relays = ways[core]
     if not relays:
-        send([(u8(T.hq[:]), [(to, u8(T.nq[:]))], far, S.an)])
-        send([(T.hs[:], [(to, T.ns[:])], far, S.an)])
+        eng = way_engines(core)
+        send([(u8(T.hq[:]), [(to, u8(T.nq[:]))], eng, S.an)])
+        send([(T.hs[:], [(to, T.ns[:])], eng, S.an)])
     else:
         R = len(relays)
         w = 256 // R
-        cut = [(j * w, j * w + w, p, far[j::R]) for j, p in enumerate(relays)]
-        send([(u8(T.hq[:, a:b]), [(p, u8(T.rq[:]))], eng, S.arel) for a, b, p, eng in cut])
-        send([(T.hs[:, a:b], [(p, T.rs[:])], eng, S.arel) for a, b, p, eng in cut])
+        cut = [(j * w, j * w + w, p, near[j::R]) for j, p in enumerate(relays)]
+        send([(u8(T.hq[:, a:b]), [(p, u8(T.rq[:]))], eng, S.arelq) for a, b, p, eng in cut])
+        send([(T.hs[:, a:b], [(p, T.rs[:])], eng, S.arels) for a, b, p, eng in cut])
     for c in on[home]:
         d, rel = ways[c]
         if core in rel:
             j, w = rel.index(core), 256 // len(rel)
-            g.wait_ge(S.arel, 2 * (E // len(rel)))
+            g.wait_ge(S.arelq, NE // len(rel))
             send([(u8(T.rq[:]), [(d, u8(T.nq[:, j * w:j * w + w]))], far, S.an)])
+            g.wait_ge(S.arels, NE // len(rel))
             send([(T.rs[:], [(d, T.ns[:, j * w:j * w + w])], far, S.an)])
     g.sem_inc(S.go2, 1)
     g.wait_ge(S.sent, sent[0])
@@ -200,8 +221,8 @@ def rank_program(g, core, T, topo):
         a, b = 128 * j, 128 * j + 128
         g.tensor.matmul_mx(T.yp[:, 512 * j:512 * j + 128], T.vq[:, 0:128], T.vs[:, 0:128], T.hq[:, a:b], T.hs[:, a:b], True, False)
     g.tensor.wait_ge(S.qv1, 1)
-    prev = cores[(rank + 1) % len(cores)]
-    g.tensor.wait_ge(S.an, 2 * E * max(1, len(ways[prev][1])))
+    nxt = cores[(rank + 1) % len(cores)]
+    g.tensor.wait_ge(S.an, 2 * (E * len(ways[nxt][1]) if ways[nxt][1] else len(way_engines(nxt))))
     for j, name in ((0, "ya"), (1, "yb")):
         a, b = 128 * j, 128 * j + 128
         g.tensor.matmul_mx(T.yp[:, 512 * j:512 * j + 128], T.vq[:, 128:256], T.vs[:, 128:256], T.nq[:, a:b], T.ns[:, a:b],

from concourse.bass import DstId, RemoteDMATransfer
from concourse.mybir import dt, AluOpType, AxisListType, ActivationFunctionType

LOADS = [(0, 1), (2, 3)]
PARTS = [(0, 1), (2, 3)]

F8, U8, F32, BF = "float8_e4m3fn_x4", "uint8", "float32", "bfloat16"
SCRATCH = {
    "xt": ("sbuf", [128, 1024], BF), "w1t": ("sbuf", [128, 2048], BF), "w2t": ("sbuf", [128, 1024], BF),
    "xq": ("sbuf", [128, 256], F8), "xs": ("sbuf", [128, 256], U8),
    "wq": ("sbuf", [128, 512], F8), "ws": ("sbuf", [128, 512], U8),
    "vq": ("sbuf", [128, 256], F8), "vs": ("sbuf", [128, 256], U8),
    "ones": ("sbuf", [128, 128], F32), "ident": ("sbuf", [128, 128], F32),
    "tops": ("sbuf", [128, 16], F32),
    "cm": ("sbuf", [128, 1], F32),
    "land": ("sbuf", [128, 4], F32),
    "rep": ("sbuf", [128, 128], F32), "rep2": ("sbuf", [128, 128], F32),
    "amax": ("sbuf", [128, 1], F32), "sc": ("sbuf", [128, 1], F32),
    "ht": ("sbuf", [128, 1024], BF),
    "hq": ("sbuf", [128, 256], F8), "hs": ("sbuf", [128, 256], U8),
    "nq": ("sbuf", [128, 256], F8), "ns": ("sbuf", [128, 256], U8),
    "rq": ("sbuf", [128, 128], F8), "rs": ("sbuf", [128, 128], U8),
    "yt": ("sbuf", [128, 256], F32),
    "z": ("psum", [128, 2048], F32), "tp": ("psum", [128, 512], F32), "yp": ("psum", [128, 1024], F32),
}
SEMAPHORES = (["ldx", "ldv", "ones", "id", "qx", "cm", "rep", "rep2", "tp", "am", "sc", "qh", "ya", "yb", "ca", "cb",
               "hout", "yout", "go1", "go2", "a1", "aon", "aoff", "arelq", "arels", "an", "sent"]
              + [s + "%d" % i for s in ("ldw", "qw", "z", "r", "h", "qv") for i in range(4)])


def bits(mask):
    return [1 << i for i in range(mask.bit_length()) if mask >> i & 1]


def plan(T, topo):
    cores = list(T.cores)
    chips = []
    for c in cores:
        if topo.chip(c) not in chips:
            chips.append(topo.chip(c))
    on = {k: [c for c in cores if topo.chip(c) == k] for k in chips}
    ports = {k: [c for c in on[k] if all(topo.may_write(c, d) for d in cores if topo.chip(d) != k)] for k in chips}
    tells = {c: [] for c in cores}
    for k in chips:
        for d in cores:
            if d in ports[k]:
                continue
            best = min(ports[k], key=lambda p: (topo.die(p) != topo.die(d), len(tells[p])))
            tells[best].append(d)
    ways = {}
    for i, c in enumerate(cores):
        d = cores[i - 1]
        ways[c] = (d, [] if topo.may_write(c, d) else ports[topo.chip(c)])
    return cores, chips, on, ports, tells, ways


def rank_program(g, core, T, topo):
    rank = T.rank_of(core)
    if rank is None:
        return
    cores, chips, on, ports, tells, ways = plan(T, topo)
    S = T.sem
    home = topo.chip(core)
    port = core in ports[home]
    k4 = 4 * on[home].index(core)
    abroad = [k for k in chips if k != home]
    far = bits(topo.mask(core, [c for c in cores if topo.chip(c) != home][0]))
    near = bits(topo.mask(core, [c for c in on[home] if c != core][0]))
    rest = [e for e in near if e not in far]
    E, NE = len(far), len(near)
    MAX, MULT = AluOpType.max, AluOpType.mult
    X = AxisListType.X
    sent = [0]

    def dst(c):
        rid, pid, _ = topo.addr(c)
        return DstId(rid=rid, pnc=pid)

    def send(transfers):
        g.remote_dma_fused([RemoteDMATransfer(dst_ids=[dst(c) for c, _ in outs], dma_engine_mask=sum(eng), remote_sem=sem,
                                              srcs=[src], dsts=[v for _, v in outs]) for src, outs, eng, sem in transfers], local_sem=S.sent)
        sent[0] += sum(len(eng) for _, _, eng, _ in transfers)

    def way_engines(c):
        m = bits(topo.mask(c, ways[c][0]))
        return [e for e in m if e not in far] if c in ports[topo.chip(c)] and len(m) > E else m

    def u8(v):
        return v.bitcast(dt.uint8)

    g.sync.dma_start(T.xt[:], T.x[:]).then_inc(S.ldx, 16)
    for n, grp in enumerate(LOADS):
        a, b = 512 * grp[0], 512 * grp[-1] + 512
        (g.sync if n % 2 else g.scalar).dma_start(T.w1t[:, a:b], T.w1[:, a:b]).then_inc(S["ldw%d" % n], 16)

    g.vector.memset(T.ones[:], 1.0).then_inc(S.ones, 1)
    g.wait_ge(S.ones, 1)
    g.affine_select(T.ident[:], T.ones[:], [[-1, 128]], AluOpType.is_equal, 0.0, 0, 1).then_inc(S.id, 1)

    g.vector.wait_ge(S.ldx, 16)
    g.vector.quantize_mx(T.xq[:], T.xs[:], T.xt[:]).then_inc(S.qx, 1)
    g.tensor.wait_ge(S.qx, 1)

    def largest(i):
        g.vector.wait_ge(S["z%d" % i], 1)
        g.vector.tensor_reduce(T.tops[:, k4 + i:k4 + i + 1], T.z[:, 512 * i:512 * i + 256], X, MAX,
                               apply_absolute_value=True).then_inc(S["r%d" % i], 1)

    late = []
    for n, grp in enumerate(LOADS):
        g.vector.wait_ge(S["ldw%d" % n], 16)
        for i in grp:
            a, b = 128 * i, 128 * i + 128
            g.vector.quantize_mx(T.wq[:, a:b], T.ws[:, a:b], T.w1t[:, 4 * a:4 * b]).then_inc(S["qw%d" % i], 1)
            g.tensor.wait_ge(S["qw%d" % i], 1)
            g.tensor.matmul_mx(T.z[:, 512 * i:512 * i + 256], T.wq[:, a:b], T.ws[:, a:b], T.xq[:], T.xs[:], True, True).then_inc(S["z%d" % i], 1)
            late.append(i)
        while late and (len(grp) > 1 or len(late) > 1):
            largest(late.pop(0))
    for i in late:
        largest(i)

    for grp in PARTS:
        for i in grp:
            g.wait_ge(S["r%d" % i], 1)
        v = T.tops[:, k4 + grp[0]:k4 + grp[-1] + 1]
        send([(v, [(p, v) for p in ports[home] if p != core], near, S.a1)])

    ci = chips.index(home)
    if port:
        for i in range(4):
            g.vector.wait_ge(S["r%d" % i], 1)
        g.vector.wait_ge(S.a1, len(PARTS) * NE * (len(on[home]) - 1))
        g.vector.tensor_reduce(T.cm[:], T.tops[:, 0:4 * len(on[home])], X, MAX).then_inc(S.cm, 1)
        g.wait_ge(S.cm, 1)
        col = T.land[:, ci:ci + 1]
        off = [d for d in tells[core] if topo.chip(d) != home]
        first = [d for d in off if ways[d][1]]
        here = [(T.cm[:], [(d, col)], rest, S.aon) for d in tells[core] if topo.chip(d) == home]
        for some in (first, [d for d in off if d not in first]):
            if some:
                send([(T.cm[:], [(d, col) for d in some], far, S.aoff)] + here)
                here = []
    g.sem_inc(S.go1, 1)

    g.sync.wait_ge(S.go1, 1)
    g.sync.dma_start(T.w2t[:], T.w2[:]).then_inc(S.ldv, 16)

    def quantise_w2():
        g.vector.wait_ge(S.ldv, 16)
        for i in range(2):
            g.vector.quantize_mx(T.vq[:, 128 * i:128 * i + 128], T.vs[:, 128 * i:128 * i + 128],
                                 T.w2t[:, 512 * i:512 * i + 512]).then_inc(S["qv%d" % i], 1)

    g.vector.wait_ge(S.ones, 1)
    if port:
        g.vector.wait_ge(S.cm, 1)
        g.vector.tensor_scalar(T.rep[:], T.ones[:], T.cm[:], None, MULT).then_inc(S.rep, 1)
    else:
        quantise_w2()
        g.vector.wait_ge(S.aon, len(rest))
        g.vector.tensor_scalar(T.rep[:], T.ones[:], T.land[:, ci:ci + 1], None, MULT).then_inc(S.rep, 1)
    g.vector.wait_ge(S.rep, 1)
    g.vector.wait_ge(S.aoff, E * len(abroad))
    c0, c1 = [chips.index(k) for k in abroad]
    g.vector.tensor_scalar(T.rep2[:], T.rep[:], T.land[:, c0:c0 + 1], T.land[:, c1:c1 + 1], MAX, MAX).then_inc(S.rep2, 1)
    g.tensor.wait_ge(S.id, 1)
    g.tensor.wait_ge(S.rep2, 1)
    g.tensor.transpose(T.tp[:, 0:128], T.rep2[:], T.ident[:]).then_inc(S.tp, 1)
    g.vector.wait_ge(S.tp, 1)
    g.vector.tensor_reduce(T.amax[:], T.tp[:, 0:128], X, MAX).then_inc(S.am, 1)
    g.vector.wait_ge(S.am, 1)
    g.vector.reciprocal(T.sc[:], T.amax[:]).then_inc(S.sc, 1)

    for b in range(2, 4):
        g.scalar.wait_ge(S["z%d" % b], 1)
    g.scalar.wait_ge(S.sc, 1)
    g.vector.wait_ge(S.sc, 1)
    for b in range(2):
        g.vector.tensor_scalar(T.ht[:, b:1024:4], T.z[:, 512 * b:512 * b + 256], T.sc[:], None, MULT).then_inc(S["h%d" % b], 1)
    for b in range(2, 4):
        g.scalar.activation(T.ht[:, b:1024:4], T.z[:, 512 * b:512 * b + 256], ActivationFunctionType.Copy,
                            scale=T.sc[:]).then_inc(S["h%d" % b], 1)
    for b in range(4):
        g.vector.wait_ge(S["h%d" % b], 1)
    g.vector.quantize_mx(T.hq[:], T.hs[:], T.ht[:]).then_inc(S.qh, 1)
    if port:
        quantise_w2()

    g.wait_ge(S.qh, 1)
    to, relays = ways[core]
    if not relays:
        eng = way_engines(core)
        send([(u8(T.hq[:]), [(to, u8(T.nq[:]))], eng, S.an)])
        send([(T.hs[:], [(to, T.ns[:])], eng, S.an)])
    else:
        R = len(relays)
        w = 256 // R
        cut = [(j * w, j * w + w, p, near[j::R]) for j, p in enumerate(relays)]
        send([(u8(T.hq[:, a:b]), [(p, u8(T.rq[:]))], eng, S.arelq) for a, b, p, eng in cut])
        send([(T.hs[:, a:b], [(p, T.rs[:])], eng, S.arels) for a, b, p, eng in cut])
    for c in on[home]:
        d, rel = ways[c]
        if core in rel:
            j, w = rel.index(core), 256 // len(rel)
            g.wait_ge(S.arelq, NE // len(rel))
            send([(u8(T.rq[:]), [(d, u8(T.nq[:, j * w:j * w + w]))], far, S.an)])
            g.wait_ge(S.arels, NE // len(rel))
            send([(T.rs[:], [(d, T.ns[:, j * w:j * w + w])], far, S.an)])
    g.sem_inc(S.go2, 1)
    g.wait_ge(S.sent, sent[0])

    g.sync.wait_ge(S.qh, 1)
    g.sync.wait_ge(S.go2, 1)
    g.sync.dma_start(T.h[:], T.ht[:]).then_inc(S.hout, 16)
    g.sync.wait_ge(S.hout, 16)

    g.tensor.wait_ge(S.qh, 1)
    g.tensor.wait_ge(S.qv0, 1)
    for j in range(2):
        a, b = 128 * j, 128 * j + 128
        g.tensor.matmul_mx(T.yp[:, 512 * j:512 * j + 128], T.vq[:, 0:128], T.vs[:, 0:128], T.hq[:, a:b], T.hs[:, a:b], True, False)
    g.tensor.wait_ge(S.qv1, 1)
    nxt = cores[(rank + 1) % len(cores)]
    g.tensor.wait_ge(S.an, 2 * (E * len(ways[nxt][1]) if ways[nxt][1] else len(way_engines(nxt))))
    for j, name in ((0, "ya"), (1, "yb")):
        a, b = 128 * j, 128 * j + 128
        g.tensor.matmul_mx(T.yp[:, 512 * j:512 * j + 128], T.vq[:, 128:256], T.vs[:, 128:256], T.nq[:, a:b], T.ns[:, a:b],
                           False, True).then_inc(S[name], 1)
    g.vector.wait_ge(S.ya, 1)
    g.vector.tensor_copy(T.yt[:, 0:128], T.yp[:, 0:128]).then_inc(S.ca, 1)
    g.scalar.wait_ge(S.yb, 1)
    g.scalar.activation(T.yt[:, 128:256], T.yp[:, 512:640], ActivationFunctionType.Copy).then_inc(S.cb, 1)
    g.scalar.wait_ge(S.ca, 1)
    g.scalar.wait_ge(S.cb, 1)
    g.scalar.dma_start(T.y[:], T.yt[:]).then_inc(S.yout, 16)
    g.scalar.wait_ge(S.yout, 16)
